import numpy as np, ml_dtypes
CORES = [2,6,10,14,18,22,26,30,34,38,42,46,50,54,58,62,66,70,74,78,82,86,90,94,98,102,106,110,114,118,122,126]
N = 32
GROUPS = [[0,1,2,3],[4,5,6,7],[8,9,10,11],[12,13,14,15],[16,17,18,19],[20,21,22,23],[24,25,26,27],[28,29,30,31]]
def setup_inputs(rng):
    return {"x": rng.standard_normal((N, 128, 16), dtype=np.float32).astype(ml_dtypes.bfloat16)}
def reference(x):
    y = np.empty((N, 128, 64), x.dtype)
    for g in GROUPS:
        s = np.concatenate([x[r] for r in g], axis=1)
        for r in g:
            y[r] = s
    return {"y": y}

@@ -1,0 +1,57 @@
+import concourse.bass as bass
+
+SCRATCH = {
+    "gather": ("sbuf", [128, 64], "bfloat16"),
+}
+SEMAPHORES = ["local", "arrived"]
+
+
+def popcount(m):
+    return bin(m).count("1")
+
+
+def split_engines(first, count, parts):
+    if parts == 0:
+        return []
+    share = count
+    while share * parts > count:
+        share //= 2
+    return [((1 << share) - 1) << (first + i * share) for i in range(parts)]
+
+
+def plan(src, members, topo):
+    peers = [c for c in members if c != src]
+    near = [c for c in peers if topo.chip(c) == topo.chip(src)]
+    far = [c for c in peers if topo.chip(c) != topo.chip(src)]
+    return list(zip(far, split_engines(0, 8, len(far)))) + list(zip(near, split_engines(8, 8, len(near))))
+
+
+def rank_program(g, core, T, topo):
+    rank = T.rank_of(core)
+    if rank is None:
+        return
+    group = [grp for grp in T.tables["GROUPS"] if rank in grp][0]
+    members = [T.cores[r] for r in group]
+    p = group.index(rank)
+    w = T.x.shape[1]
+    mine = T.gather[:, p * w:(p + 1) * w]
+
+    g.dma_start(mine, T.x[:]).then_inc(T.sem.local, 16)
+    g.wait_ge(T.sem.local, 16)
+
+    transfers = []
+    for dst, m in plan(core, members, topo):
+        rid, pid = topo.addr(dst)[:2]
+        transfers.append(bass.RemoteDMATransfer(
+            dst_ids=[bass.DstId(rid=rid, pnc=pid)], dma_engine_mask=m, remote_sem=T.sem.arrived,
+            src=mine, dst=mine))
+    g.remote_dma_fused(transfers, local_sem=T.sem.arrived)
+
+    total = sum(popcount(m) for d, m in plan(core, members, topo))
+    for c in members:
+        if c != core:
+            total += sum(popcount(m) for d, m in plan(c, members, topo) if d == core)
+    g.wait_ge(T.sem.arrived, total)
+
+    g.dma_start(T.y[:], T.gather[:]).then_inc(T.sem.local, 16)
+    g.wait_ge(T.sem.local, 32)

@@ -3,7 +3,7 @@ import concourse.bass as bass
 SCRATCH = {
     "gather": ("sbuf", [128, 64], "bfloat16"),
 }
-SEMAPHORES = ["local", "arrived"]
+SEMAPHORES = ["local", "arrived", "sent"]
 
 
 def popcount(m):
@@ -45,13 +45,15 @@ def rank_program(g, core, T, topo):
         transfers.append(bass.RemoteDMATransfer(
             dst_ids=[bass.DstId(rid=rid, pnc=pid)], dma_engine_mask=m, remote_sem=T.sem.arrived,
             src=mine, dst=mine))
-    g.remote_dma_fused(transfers, local_sem=T.sem.arrived)
+    g.remote_dma_fused(transfers, local_sem=T.sem.sent)
 
-    total = sum(popcount(m) for d, m in plan(core, members, topo))
+    incoming = 0
     for c in members:
         if c != core:
-            total += sum(popcount(m) for d, m in plan(c, members, topo) if d == core)
-    g.wait_ge(T.sem.arrived, total)
+            incoming += sum(popcount(m) for d, m in plan(c, members, topo) if d == core)
+    g.wait_ge(T.sem.arrived, incoming)
 
     g.dma_start(T.y[:], T.gather[:]).then_inc(T.sem.local, 16)
+
+    g.wait_ge(T.sem.sent, sum(popcount(m) for d, m in plan(core, members, topo)))
     g.wait_ge(T.sem.local, 32)

import concourse.bass as bass

SCRATCH = {
    "gather": ("sbuf", [128, 64], "bfloat16"),
}
SEMAPHORES = ["local", "arrived", "sent"]


def popcount(m):
    return bin(m).count("1")


def split_engines(first, count, parts):
    if parts == 0:
        return []
    share = count
    while share * parts > count:
        share //= 2
    return [((1 << share) - 1) << (first + i * share) for i in range(parts)]


def plan(src, members, topo):
    peers = [c for c in members if c != src]
    near = [c for c in peers if topo.chip(c) == topo.chip(src)]
    far = [c for c in peers if topo.chip(c) != topo.chip(src)]
    return list(zip(far, split_engines(0, 8, len(far)))) + list(zip(near, split_engines(8, 8, len(near))))


def rank_program(g, core, T, topo):
    rank = T.rank_of(core)
    if rank is None:
        return
    group = [grp for grp in T.tables["GROUPS"] if rank in grp][0]
    members = [T.cores[r] for r in group]
    p = group.index(rank)
    w = T.x.shape[1]
    mine = T.gather[:, p * w:(p + 1) * w]

    g.dma_start(mine, T.x[:]).then_inc(T.sem.local, 16)
    g.wait_ge(T.sem.local, 16)

    transfers = []
    for dst, m in plan(core, members, topo):
        rid, pid = topo.addr(dst)[:2]
        transfers.append(bass.RemoteDMATransfer(
            dst_ids=[bass.DstId(rid=rid, pnc=pid)], dma_engine_mask=m, remote_sem=T.sem.arrived,
            src=mine, dst=mine))
    g.remote_dma_fused(transfers, local_sem=T.sem.sent)

    incoming = 0
    for c in members:
        if c != core:
            incoming += sum(popcount(m) for d, m in plan(c, members, topo) if d == core)
    g.wait_ge(T.sem.arrived, incoming)

    g.dma_start(T.y[:], T.gather[:]).then_inc(T.sem.local, 16)

    g.wait_ge(T.sem.sent, sum(popcount(m) for d, m in plan(core, members, topo)))
    g.wait_ge(T.sem.local, 32)
